import numpy as np
import ml_dtypes


def mxq(x, axis, fmt="e4m3"):
    dtype, down = {"e4m3": (ml_dtypes.float8_e4m3fn, 7), "e5m2": (ml_dtypes.float8_e5m2, 14)}[fmt]
    v = np.moveaxis(np.asarray(x, np.float32).astype(ml_dtypes.bfloat16).astype(np.float64), axis, -1)
    blocks = v.reshape(v.shape[:-1] + (-1, 32))
    amax = np.abs(blocks).max(-1, keepdims=True)
    byte = np.maximum(np.where(amax > 0, np.frexp(amax)[1] - 1 + 127, 0) - down, 1)
    scale = np.exp2(byte - 127.0)
    codes = (blocks / scale).astype(np.float32).astype(dtype).astype(np.float64)
    return np.moveaxis((codes * scale).reshape(v.shape), -1, axis)


WIDE = False


def mx_kscale(k):
    if not WIDE:
        return np.ones(k)
    levels = np.array([10, -10, 5, -5, 0])
    if k % 512:
        return np.exp2(np.random.permutation(np.resize(levels, k // 32))).repeat(32)
    a = np.empty((k // 512, 16))
    for p in range(k // 512):
        a[p, :8] = np.random.permutation(np.resize(levels, 8))
        for g in range(8):
            far = levels[np.abs(levels - a[p, g]) >= 10]
            a[p, g + 8] = far[np.random.randint(len(far))]
    return np.exp2(a.ravel()).repeat(32)


def f64(x):
    return np.asarray(x).astype(np.float64)


def striped(idx):
    return np.tile(np.asarray(idx).reshape(-1, 16).T, (8, 1)).astype(np.uint16)


def unstriped(offs):
    return offs[:16].T.reshape(-1).astype(np.int64)


E2M1 = np.array([0.0, 0.5, 1.0, 1.5, 2.0, 3.0, 4.0, 6.0, -0.0, -0.5, -1.0, -1.5, -2.0, -3.0, -4.0, -6.0])


def pack_weight(w, fmt):
    k, n = w.shape
    w = f64(np.asarray(w, np.float32).astype(ml_dtypes.bfloat16)).reshape(k // 32, 32, n)
    amax = np.abs(w).max(1)
    if fmt == "e4m3":
        byte = np.frexp(amax)[1] - 1 + 127 - 7
    else:
        mant, ex = np.frexp(amax / 6.0)
        byte = np.where(mant > 0.5, ex, ex - 1) + 127
    byte = np.clip(np.where(amax > 0, byte, 1), 1, 254)
    scaled = (w * np.exp2(127.0 - byte)[:, None, :]).reshape(k, n).astype(np.float32)
    by_word = np.ascontiguousarray(scaled.reshape(k // 512, 128, 4, n).transpose(0, 1, 3, 2))
    if fmt == "e4m3":
        words = by_word.astype(ml_dtypes.float8_e4m3fn).view(np.uint8)
    else:
        c = by_word.astype(ml_dtypes.float4_e2m1fn).view(np.uint8) & 0xF
        words = (c[..., 0::2] | (c[..., 1::2] << 4)).reshape(k // 512, 128, 2 * n)
    return np.ascontiguousarray(words), np.ascontiguousarray(byte.astype(np.uint8).reshape(k // 512, 16, n))


def unpack_weight(words, scales, fmt):
    g, _, n = scales.shape
    words = np.ascontiguousarray(words).reshape(g, 128, n, -1)
    if fmt == "e4m3":
        vals = words.view(ml_dtypes.float8_e4m3fn).astype(np.float64)
    else:
        nib = np.empty((g, 128, n, 4), np.uint8)
        nib[..., 0::2] = words & 0xF
        nib[..., 1::2] = words >> 4
        vals = E2M1[nib]
    vals = vals * np.repeat(np.exp2(scales.astype(np.float64) - 127.0), 8, axis=1)[..., None]
    return vals.transpose(0, 1, 3, 2).reshape(g * 512, n)


D, E, T, I, G, U, Q = 512, 512, 4096, 1024, 64, 512, 128


def setup_inputs():
    n = np.random.standard_normal
    idx = np.random.permutation(T)[:I]
    idx2 = np.random.permutation(U)[:G]
    fd = mx_kscale(D)
    fe = mx_kscale(E)
    keysp = pack_weight(n((D, T)) / fd[:, None], "e2m1")
    valsp = pack_weight(n((E, T)) / fe[:, None], "e2m1")
    return {
        "query": (n((D, Q)) * 0.6 / np.sqrt(D) * fd[:, None]).astype(np.float32),
        "keys_words": keysp[0],
        "keys_scales": keysp[1],
        "gout": (n((E, Q)) * 1 / np.sqrt(E) * fe[:, None]).astype(np.float32),
        "vals_words": valsp[0],
        "vals_scales": valsp[1],
        "old": (np.random.uniform(0.0, 8.0, (Q, U))).astype(np.float32),
        "fade": (np.random.uniform(0.5, 1.0, (1, U))).astype(np.float32),
        "offs": striped(idx),
        "offs2": striped(idx2),
    }


def reference(query, keys_words, keys_scales, gout, vals_words, vals_scales, old, fade, offs, offs2):
    idx = unstriped(offs)
    idx2 = unstriped(offs2)
    keysu = unpack_weight(keys_words, keys_scales, "e2m1")
    valsu = unpack_weight(vals_words, vals_scales, "e2m1")
    queryq = mxq(f64(query), 0, "e4m3")
    keysidxg = keysu[:, idx]
    a = queryq.T @ keysidxg
    goutq = mxq(f64(gout), 0, "e4m3")
    valsidxg = valsu[:, idx]
    dp = goutq.T @ valsidxg
    p = np.exp(a - np.max(a, axis=1, keepdims=True))
    sg = (p * np.abs(dp)).reshape(Q, G, I // G).sum(axis=2) / np.sum(p, axis=1, keepdims=True) * 512.0
    sf = np.zeros((Q, U))
    sf[:, idx2] = sg
    y = f64(old) * f64(fade) + sf
    return y

@@ -1,0 +1,161 @@
+from contextlib import ExitStack
+
+import concourse.mybir as mybir
+from concourse.masks import make_identity
+
+D, E, T, I, G, U, Q = 512, 512, 4096, 1024, 64, 512, 128
+FLOPS = 2 * Q * I * (D + E)
+
+F32 = mybir.dt.float32
+BF16 = mybir.dt.bfloat16
+I32 = mybir.dt.int32
+U32 = mybir.dt.uint32
+U16 = mybir.dt.uint16
+U8 = mybir.dt.uint8
+FP8X4 = mybir.dt.float8_e4m3fn_x4
+FP4X4 = mybir.dt.float4_e2m1fn_x4
+ALU = mybir.AluOpType
+ACT = mybir.ActivationFunctionType
+AX = mybir.AxisListType
+
+P = 128
+PACK = 4
+HALF = 512
+PAGE = I // G
+ROWS = 16
+
+
+def tile_attend_pagesaliency_kernel(tc, query, keys_words, keys_scales, gout, vals_words, vals_scales,
+                                     old, fade, offs, offs2, out):
+    nc = tc.nc
+    with ExitStack() as ctx:
+        keep = ctx.enter_context(tc.tile_pool(name="keep", bufs=1))
+        psum = ctx.enter_context(tc.psum_pool(name="psum", bufs=1))
+
+        slots = keep.tile([P, I // 16], U16, name="slots")
+        pages = keep.tile([P, G // 16], U16, name="pages")
+        nc.sync.dma_start(slots[:], offs)
+
+        def load_scales(src, name):
+            pool_bytes = keep.tile([P, T], U8, name=name, align_bytes=64)
+            rows = src[0].bitcast(I32)
+            nc.sync.dma_start(pool_bytes[0:32, :].bitcast(I32), rows.unsqueeze(1).to_broadcast([ROWS, 2, T // 4]))
+            nc.vector.memset(pool_bytes[32:64, :].bitcast(I32), 0)
+            nc.vector.memset(pool_bytes[64:128, :].bitcast(I32), 0)
+            return pool_bytes
+
+        def load_words(src, name):
+            pool_words = keep.tile([P, T], U16, name=name, align_bytes=64)
+            nc.sync.dma_start(pool_words[:].bitcast(I32), src[0].bitcast(I32))
+            return pool_words
+
+        def load_rows(src, name):
+            raw = keep.tile([P, PACK, Q], F32, name=name)
+            nc.sync.dma_start(raw[:], src.rearrange("(p j) q -> p j q", j=PACK))
+            return raw
+
+        k_bytes = load_scales(keys_scales, "k_bytes")
+        v_bytes = load_scales(vals_scales, "v_bytes")
+        k_words = load_words(keys_words, "k_words")
+        q_raw = load_rows(query, "q_raw")
+        g_raw = load_rows(gout, "g_raw")
+        v_words = load_words(vals_words, "v_words")
+        old_sb = keep.tile([P, U], F32, name="old_sb")
+        nc.sync.dma_start(old_sb[:], old)
+        fade_col = keep.tile([P, U // P], F32, name="fade_col")
+        with nc.allow_non_contiguous_dma(reason="one fade value to a partition"):
+            nc.sync.dma_start(fade_col[:], fade.rearrange("o (c p) -> p (o c)", p=P))
+        nc.sync.dma_start(pages[:], offs2)
+
+        warm = keep.tile([P, 1], F32, name="warm")
+        warm_out = keep.tile([P, 1], F32, name="warm_out")
+        nc.gpsimd.memset(warm[:], 0.0)
+        nc.scalar.activation(warm_out[:], warm[:], ACT.Exp)
+
+        ident = keep.tile([P, P], F32, name="ident")
+        make_identity(nc, ident[:])
+        placed = keep.tile([P, U], F32, name="placed")
+        nc.gpsimd.memset(placed[:], 0.0)
+
+        def gather_scales(pool_bytes, name):
+            picked = keep.tile([P, I], U8, name=name + "_picked", align_bytes=64)
+            nc.vector.tensor_copy(picked[:], pool_bytes[:].indirect(slots[:]))
+            plane = keep.tile([P, I], U8, name=name + "_plane", align_bytes=64)
+            for j in range(4):
+                nc.sync.dma_start(plane[j:P:4, :].bitcast(I32), picked[2 * j:2 * j + 32, :].bitcast(I32))
+            return plane
+
+        def gather_words(pool_words, h, name):
+            picked = keep.tile([P, HALF], U16, name=name, align_bytes=64)
+            cols = slice(h * HALF // 16, (h + 1) * HALF // 16)
+            nc.vector.tensor_copy(picked[:], pool_words[:].indirect(slots[:, cols]))
+            return picked
+
+        k_plane = gather_scales(k_bytes, "k")
+        v_plane = gather_scales(v_bytes, "v")
+
+        grouped = keep.tile([P, 2, Q, PACK], BF16, name="grouped", align_bytes=64)
+        nc.scalar.copy(grouped[:, 0], q_raw[:].rearrange("p j q -> p q j"))
+        nc.scalar.copy(grouped[:, 1], g_raw[:].rearrange("p j q -> p q j"))
+        codes = keep.tile([P, 2 * Q], U32, name="codes", align_bytes=64)
+        scales = keep.tile([P, 2 * Q], U8, name="scales", align_bytes=64)
+        nc.vector.quantize_mx(out=codes[:].bitcast(FP8X4), scales=scales[:],
+                              in_=grouped[:].rearrange("p s q j -> p (s q j)"))
+
+        def product(side, picked, plane, h, name):
+            bank = psum.tile([P, HALF], F32, name=name)
+            rows = slice(side * Q, (side + 1) * Q)
+            nc.tensor.matmul_mx(out=bank[:], lhsT=codes[:, rows].bitcast(FP8X4), lhsT_scale=scales[:, rows],
+                                rhs=picked[:].bitcast(FP4X4), rhs_scale=plane[:, h * HALF:(h + 1) * HALF],
+                                start=True, stop=True)
+            return bank
+
+        a = [product(0, gather_words(k_words, h, "k_pick%d" % h), k_plane, h, "a%d" % h) for h in range(2)]
+
+        neg0 = keep.tile([P, 1], F32, name="neg0")
+        neg = keep.tile([P, 1], F32, name="neg")
+        negated = keep.tile([P, HALF], F32, name="negated")
+        nc.vector.tensor_reduce(neg0[:], a[0][:], AX.X, ALU.max, negate=True)
+        nc.vector.tensor_scalar(negated[:], a[1][:], -1.0, neg0[:], ALU.mult, ALU.min, accum_out=neg[:])
+
+        p = []
+        sums = []
+        for h in range(2):
+            ph = keep.tile([P, HALF], F32, name="p%d" % h)
+            sh = keep.tile([P, 1], F32, name="sum%d" % h)
+            nc.scalar.activation(ph[:], a[h][:], ACT.Exp, bias=neg[:], accum_out=sh[:])
+            p.append(ph)
+            sums.append(sh)
+        total = keep.tile([P, 1], F32, name="total")
+        nc.scalar.activation(total[:], sums[0][:], ACT.Identity, bias=sums[1][:])
+        inv = keep.tile([P, 1], F32, name="inv")
+        nc.vector.reciprocal(inv[:], total[:])
+        factor = keep.tile([P, G], F32, name="factor")
+        nc.scalar.activation(factor[:], inv[:].to_broadcast([P, G]), ACT.Copy, scale=512.0)
+
+        turned = psum.tile([P, U // P, P], F32, name="turned")
+        faded_t = keep.tile([P, U // P, P], F32, name="faded_t")
+        faded = psum.tile([P, U], F32, name="faded")
+        for c in range(U // P):
+            nc.tensor.transpose(turned[:, c, :], old_sb[:, c * P:(c + 1) * P], ident[:])
+        for c in range(U // P):
+            nc.scalar.activation(faded_t[:, c, :], turned[:, c, :], ACT.Copy, scale=fade_col[:, c:c + 1])
+        for c in range(U // P):
+            nc.tensor.transpose(faded[:, c * P:(c + 1) * P], faded_t[:, c, :], ident[:])
+
+        dp = [product(1, gather_words(v_words, h, "v_pick%d" % h), v_plane, h, "dp%d" % h) for h in range(2)]
+
+        page_sum = keep.tile([P, G], F32, name="page_sum")
+        for h in range(2):
+            w = keep.tile([P, HALF], F32, name="w%d" % h)
+            nc.vector.tensor_tensor(w[:], dp[h][:], p[h][:], ALU.mult)
+            nc.vector.tensor_reduce(page_sum[:, h * G // 2:(h + 1) * G // 2],
+                                    w[:].rearrange("q (g s) -> q g s", s=PAGE), AX.X, ALU.add,
+                                    apply_absolute_value=True)
+        nc.vector.tensor_tensor(placed[:].indirect(pages[:]), page_sum[:], factor[:], ALU.mult)
+
+        for h in range(2):
+            cols = slice(h * U // 2, (h + 1) * U // 2)
+            res = keep.tile([P, U // 2], F32, name="res%d" % h)
+            nc.vector.tensor_tensor(res[:], faded[:, cols], placed[:, cols], ALU.add)
+            (nc.sync if h == 0 else nc.scalar).dma_start(out[:, cols], res[:])

@@ -36,35 +36,28 @@ def tile_attend_pagesaliency_kernel(tc, query, keys_words, keys_scales, gout, va
         pages = keep.tile([P, G // 16], U16, name="pages")
         nc.sync.dma_start(slots[:], offs)
 
-        def load_scales(src, name):
-            pool_bytes = keep.tile([P, T], U8, name=name, align_bytes=64)
-            rows = src[0].bitcast(I32)
-            nc.sync.dma_start(pool_bytes[0:32, :].bitcast(I32), rows.unsqueeze(1).to_broadcast([ROWS, 2, T // 4]))
-            nc.vector.memset(pool_bytes[32:64, :].bitcast(I32), 0)
-            nc.vector.memset(pool_bytes[64:128, :].bitcast(I32), 0)
-            return pool_bytes
-
         def load_words(src, name):
             pool_words = keep.tile([P, T], U16, name=name, align_bytes=64)
-            nc.sync.dma_start(pool_words[:].bitcast(I32), src[0].bitcast(I32))
+            nc.scalar.dma_start(pool_words[:].bitcast(I32), src[0].bitcast(I32))
             return pool_words
 
         def load_rows(src, name):
             raw = keep.tile([P, PACK, Q], F32, name=name)
-            nc.sync.dma_start(raw[:], src.rearrange("(p j) q -> p j q", j=PACK))
+            nc.scalar.dma_start(raw[:], src.rearrange("(p j) q -> p j q", j=PACK))
             return raw
 
-        k_bytes = load_scales(keys_scales, "k_bytes")
-        v_bytes = load_scales(vals_scales, "v_bytes")
-        k_words = load_words(keys_words, "k_words")
+        k_bytes = keep.tile([P, T], U8, name="k_bytes", tag="k_bytes", align_bytes=64)
+        nc.scalar.dma_start(k_bytes[0:32, :].bitcast(I32),
+                            keys_scales[0].bitcast(I32).unsqueeze(1).to_broadcast([ROWS, 2, T // 4]))
+        nc.vector.memset(k_bytes[32:64, :].bitcast(I32), 0)
+        nc.vector.memset(k_bytes[64:128, :].bitcast(I32), 0)
+        v_bytes = keep.tile([P, T], U8, name="v_bytes", tag="v_bytes", align_bytes=64)
+        nc.scalar.dma_start(v_bytes[:].bitcast(I32),
+                            vals_scales[0].bitcast(I32).unsqueeze(1).to_broadcast([ROWS, 8, T // 4]))
         q_raw = load_rows(query, "q_raw")
+        k_words = load_words(keys_words, "k_words")
         g_raw = load_rows(gout, "g_raw")
         v_words = load_words(vals_words, "v_words")
-        old_sb = keep.tile([P, U], F32, name="old_sb")
-        nc.sync.dma_start(old_sb[:], old)
-        fade_col = keep.tile([P, U // P], F32, name="fade_col")
-        with nc.allow_non_contiguous_dma(reason="one fade value to a partition"):
-            nc.sync.dma_start(fade_col[:], fade.rearrange("o (c p) -> p (o c)", p=P))
         nc.sync.dma_start(pages[:], offs2)
 
         warm = keep.tile([P, 1], F32, name="warm")
@@ -78,45 +71,57 @@ def tile_attend_pagesaliency_kernel(tc, query, keys_words, keys_scales, gout, va
         nc.gpsimd.memset(placed[:], 0.0)
 
         def gather_scales(pool_bytes, name):
-            picked = keep.tile([P, I], U8, name=name + "_picked", align_bytes=64)
+            picked = keep.tile([P, I], U8, name=name, align_bytes=64)
             nc.vector.tensor_copy(picked[:], pool_bytes[:].indirect(slots[:]))
-            plane = keep.tile([P, I], U8, name=name + "_plane", align_bytes=64)
-            for j in range(4):
-                nc.sync.dma_start(plane[j:P:4, :].bitcast(I32), picked[2 * j:2 * j + 32, :].bitcast(I32))
-            return plane
+            return picked
 
-        def gather_words(pool_words, h, name):
-            picked = keep.tile([P, HALF], U16, name=name, align_bytes=64)
+        def gather_words(pool_words, h, name, tag):
+            picked = keep.tile([P, HALF], U16, name=name, tag=tag, align_bytes=64)
             cols = slice(h * HALF // 16, (h + 1) * HALF // 16)
             nc.vector.tensor_copy(picked[:], pool_words[:].indirect(slots[:, cols]))
             return picked
 
-        k_plane = gather_scales(k_bytes, "k")
-        v_plane = gather_scales(v_bytes, "v")
+        k_picked = gather_scales(k_bytes, "k_picked")
+        k_plane = keep.tile([P, I], U8, name="k_plane", align_bytes=64)
+        for j in range(4):
+            nc.sync.dma_start(k_plane[j:P:4, :].bitcast(I32), k_picked[2 * j:2 * j + 32, :].bitcast(I32))
+        v_picked = gather_scales(v_bytes, "v_picked")
+        v_plane = keep.tile([P, I], U8, name="v_plane", align_bytes=64)
+        nc.gpsimd.memset(v_plane[:].bitcast(I32), 0)
+        for j in range(4):
+            nc.sync.dma_start(v_plane[j:P:32, :].bitcast(I32), v_picked[8 * j:P:32, :].bitcast(I32))
 
-        grouped = keep.tile([P, 2, Q, PACK], BF16, name="grouped", align_bytes=64)
-        nc.scalar.copy(grouped[:, 0], q_raw[:].rearrange("p j q -> p q j"))
-        nc.scalar.copy(grouped[:, 1], g_raw[:].rearrange("p j q -> p q j"))
-        codes = keep.tile([P, 2 * Q], U32, name="codes", align_bytes=64)
-        scales = keep.tile([P, 2 * Q], U8, name="scales", align_bytes=64)
-        nc.vector.quantize_mx(out=codes[:].bitcast(FP8X4), scales=scales[:],
-                              in_=grouped[:].rearrange("p s q j -> p (s q j)"))
+        def quantise(raw, name):
+            grouped = keep.tile([P, Q, PACK], BF16, name=name + "_grouped", align_bytes=64)
+            nc.scalar.copy(grouped[:], raw[:].rearrange("p j q -> p q j"))
+            codes = keep.tile([P, Q], U32, name=name + "_codes", align_bytes=64)
+            scales = keep.tile([P, Q], U8, name=name + "_scales", align_bytes=64)
+            nc.vector.quantize_mx(out=codes[:].bitcast(FP8X4), scales=scales[:],
+                                  in_=grouped[:].rearrange("p q j -> p (q j)"))
+            return codes, scales
 
-        def product(side, picked, plane, h, name):
+        def product(rows, picked, plane, h, name):
             bank = psum.tile([P, HALF], F32, name=name)
-            rows = slice(side * Q, (side + 1) * Q)
-            nc.tensor.matmul_mx(out=bank[:], lhsT=codes[:, rows].bitcast(FP8X4), lhsT_scale=scales[:, rows],
+            nc.tensor.matmul_mx(out=bank[:], lhsT=rows[0][:].bitcast(FP8X4), lhsT_scale=rows[1][:],
                                 rhs=picked[:].bitcast(FP4X4), rhs_scale=plane[:, h * HALF:(h + 1) * HALF],
                                 start=True, stop=True)
             return bank
 
-        a = [product(0, gather_words(k_words, h, "k_pick%d" % h), k_plane, h, "a%d" % h) for h in range(2)]
+        q_mx = quantise(q_raw, "q")
+        a = [product(q_mx, gather_words(k_words, h, "k_pick%d" % h, "k_pick%d" % h), k_plane, h, "a%d" % h)
+             for h in range(2)]
+        g_mx = quantise(g_raw, "g")
 
         neg0 = keep.tile([P, 1], F32, name="neg0")
         neg = keep.tile([P, 1], F32, name="neg")
-        negated = keep.tile([P, HALF], F32, name="negated")
-        nc.vector.tensor_reduce(neg0[:], a[0][:], AX.X, ALU.max, negate=True)
-        nc.vector.tensor_scalar(negated[:], a[1][:], -1.0, neg0[:], ALU.mult, ALU.min, accum_out=neg[:])
+        dp = []
+        for h in range(2):
+            negated = keep.tile([P, HALF], F32, name="negated%d" % h, tag="turn%d" % h, align_bytes=64)
+            if h == 0:
+                nc.vector.tensor_scalar(negated[:], a[0][:], -1.0, None, ALU.mult, ALU.min, accum_out=neg0[:])
+            else:
+                nc.vector.tensor_scalar(negated[:], a[1][:], -1.0, neg0[:], ALU.mult, ALU.min, accum_out=neg[:])
+            dp.append(product(g_mx, gather_words(v_words, h, "v_pick%d" % h, "turn%d" % h), v_plane, h, "dp%d" % h))
 
         p = []
         sums = []
@@ -133,6 +138,11 @@ def tile_attend_pagesaliency_kernel(tc, query, keys_words, keys_scales, gout, va
         factor = keep.tile([P, G], F32, name="factor")
         nc.scalar.activation(factor[:], inv[:].to_broadcast([P, G]), ACT.Copy, scale=512.0)
 
+        old_sb = keep.tile([P, U], F32, name="old_sb", tag="v_bytes", align_bytes=64)
+        nc.sync.dma_start(old_sb[:], old)
+        fade_col = keep.tile([P, U // P], F32, name="fade_col", tag="k_bytes", align_bytes=64)
+        with nc.allow_non_contiguous_dma(reason="one fade value to a partition"):
+            nc.sync.dma_start(fade_col[:], fade.rearrange("o (c p) -> p (o c)", p=P))
         turned = psum.tile([P, U // P, P], F32, name="turned")
         faded_t = keep.tile([P, U // P, P], F32, name="faded_t")
         faded = psum.tile([P, U], F32, name="faded")
@@ -143,14 +153,15 @@ def tile_attend_pagesaliency_kernel(tc, query, keys_words, keys_scales, gout, va
         for c in range(U // P):
             nc.tensor.transpose(faded[:, c * P:(c + 1) * P], faded_t[:, c, :], ident[:])
 
-        dp = [product(1, gather_words(v_words, h, "v_pick%d" % h), v_plane, h, "dp%d" % h) for h in range(2)]
-
         page_sum = keep.tile([P, G], F32, name="page_sum")
+        w = []
         for h in range(2):
-            w = keep.tile([P, HALF], F32, name="w%d" % h)
-            nc.vector.tensor_tensor(w[:], dp[h][:], p[h][:], ALU.mult)
+            wh = keep.tile([P, HALF], F32, name="w%d" % h)
+            nc.vector.tensor_tensor(wh[:], dp[h][:], p[h][:], ALU.mult)
+            w.append(wh)
+        for h in range(2):
             nc.vector.tensor_reduce(page_sum[:, h * G // 2:(h + 1) * G // 2],
-                                    w[:].rearrange("q (g s) -> q g s", s=PAGE), AX.X, ALU.add,
+                                    w[h][:].rearrange("q (g s) -> q g s", s=PAGE), AX.X, ALU.add,
                                     apply_absolute_value=True)
         nc.vector.tensor_tensor(placed[:].indirect(pages[:]), page_sum[:], factor[:], ALU.mult)
 

@@ -36,63 +36,56 @@ def tile_attend_pagesaliency_kernel(tc, query, keys_words, keys_scales, gout, va
         pages = keep.tile([P, G // 16], U16, name="pages")
         nc.sync.dma_start(slots[:], offs)
 
-        def load_words(src, name):
-            pool_words = keep.tile([P, T], U16, name=name, align_bytes=64)
-            nc.scalar.dma_start(pool_words[:].bitcast(I32), src[0].bitcast(I32))
+        def load_words(src, name, tag):
+            pool_words = keep.tile([P, T], U16, name=name, tag=tag, align_bytes=64)
+            nc.sync.dma_start(pool_words[:].bitcast(I32), src[0].bitcast(I32))
             return pool_words
 
         def load_rows(src, name):
-            raw = keep.tile([P, PACK, Q], F32, name=name)
-            nc.scalar.dma_start(raw[:], src.rearrange("(p j) q -> p j q", j=PACK))
+            raw = keep.tile([P, PACK, Q], F32, name=name, tag=name)
+            nc.sync.dma_start(raw[:], src.rearrange("(p j) q -> p j q", j=PACK))
             return raw
 
-        k_bytes = keep.tile([P, T], U8, name="k_bytes", tag="k_bytes", align_bytes=64)
-        nc.scalar.dma_start(k_bytes[0:32, :].bitcast(I32),
-                            keys_scales[0].bitcast(I32).unsqueeze(1).to_broadcast([ROWS, 2, T // 4]))
-        nc.vector.memset(k_bytes[32:64, :].bitcast(I32), 0)
-        nc.vector.memset(k_bytes[64:128, :].bitcast(I32), 0)
         v_bytes = keep.tile([P, T], U8, name="v_bytes", tag="v_bytes", align_bytes=64)
-        nc.scalar.dma_start(v_bytes[:].bitcast(I32),
-                            vals_scales[0].bitcast(I32).unsqueeze(1).to_broadcast([ROWS, 8, T // 4]))
-        q_raw = load_rows(query, "q_raw")
-        k_words = load_words(keys_words, "k_words")
-        g_raw = load_rows(gout, "g_raw")
-        v_words = load_words(vals_words, "v_words")
+        nc.sync.dma_start(v_bytes[0:32, :].bitcast(I32),
+                          vals_scales[0].bitcast(I32).unsqueeze(1).to_broadcast([ROWS, 2, T // 4]))
         nc.sync.dma_start(pages[:], offs2)
+        k_words = load_words(keys_words, "k_words", "k_words")
+        q_raw = load_rows(query, "q_raw")
+        g_raw = load_rows(gout, "g_raw")
+        old_sb = keep.tile([P, U], F32, name="old_sb")
+        nc.sync.dma_start(old_sb[:], old)
 
-        warm = keep.tile([P, 1], F32, name="warm")
-        warm_out = keep.tile([P, 1], F32, name="warm_out")
-        nc.gpsimd.memset(warm[:], 0.0)
+        warm = keep.tile([P, 1], F32, name="warm", tag="warm")
+        warm_out = keep.tile([P, 1], F32, name="warm_out", tag="warm_out")
+        nc.vector.memset(warm[:], 0.0)
         nc.scalar.activation(warm_out[:], warm[:], ACT.Exp)
-
-        ident = keep.tile([P, P], F32, name="ident")
+        k_bytes = keep.tile([P, T], U8, name="k_bytes", tag="k_bytes", align_bytes=64)
+        nc.vector.memset(k_bytes[:].bitcast(I32), 0)
+        for j in range(4):
+            nc.scalar.dma_start(k_bytes[j:P:32, :].bitcast(I32), keys_scales[0, j:ROWS:4, :].bitcast(I32))
+        nc.vector.memset(v_bytes[32:64, :].bitcast(I32), 0)
+        nc.vector.memset(v_bytes[64:128, :].bitcast(I32), 0)
+        ident = keep.tile([P, P], F32, name="ident", tag="warm_out")
         make_identity(nc, ident[:])
-        placed = keep.tile([P, U], F32, name="placed")
-        nc.gpsimd.memset(placed[:], 0.0)
+        fade_col = keep.tile([P, U // P], F32, name="fade_col", tag="warm")
+        with nc.allow_non_contiguous_dma(reason="one fade value to a partition"):
+            nc.gpsimd.dma_start(fade_col[:], fade.rearrange("o (c p) -> p (o c)", p=P))
 
-        def gather_scales(pool_bytes, name):
-            picked = keep.tile([P, I], U8, name=name, align_bytes=64)
-            nc.vector.tensor_copy(picked[:], pool_bytes[:].indirect(slots[:]))
-            return picked
+        def half_list(h):
+            return slots[:, h * HALF // 16:(h + 1) * HALF // 16]
 
-        def gather_words(pool_words, h, name, tag):
-            picked = keep.tile([P, HALF], U16, name=name, tag=tag, align_bytes=64)
-            cols = slice(h * HALF // 16, (h + 1) * HALF // 16)
-            nc.vector.tensor_copy(picked[:], pool_words[:].indirect(slots[:, cols]))
-            return picked
-
-        k_picked = gather_scales(k_bytes, "k_picked")
-        k_plane = keep.tile([P, I], U8, name="k_plane", align_bytes=64)
-        for j in range(4):
-            nc.sync.dma_start(k_plane[j:P:4, :].bitcast(I32), k_picked[2 * j:2 * j + 32, :].bitcast(I32))
-        v_picked = gather_scales(v_bytes, "v_picked")
+        v_picked = keep.tile([P, I], U8, name="v_picked", align_bytes=64)
+        nc.vector.tensor_copy(v_picked[:], v_bytes[:].indirect(slots[:]))
+        v_words = load_words(vals_words, "v_words", "v_bytes")
         v_plane = keep.tile([P, I], U8, name="v_plane", align_bytes=64)
-        nc.gpsimd.memset(v_plane[:].bitcast(I32), 0)
         for j in range(4):
-            nc.sync.dma_start(v_plane[j:P:32, :].bitcast(I32), v_picked[8 * j:P:32, :].bitcast(I32))
+            nc.sync.dma_start(v_plane[j:P:4, :].bitcast(I32), v_picked[2 * j:2 * j + 32, :].bitcast(I32))
+        k_pick = keep.tile([P, I], U16, name="k_pick", align_bytes=64)
+        nc.vector.tensor_copy(k_pick[:], k_words[:].indirect(slots[:]))
 
         def quantise(raw, name):
-            grouped = keep.tile([P, Q, PACK], BF16, name=name + "_grouped", align_bytes=64)
+            grouped = keep.tile([P, Q, PACK], BF16, name=name + "_grouped", tag=name + "_grouped", align_bytes=64)
             nc.scalar.copy(grouped[:], raw[:].rearrange("p j q -> p q j"))
             codes = keep.tile([P, Q], U32, name=name + "_codes", align_bytes=64)
             scales = keep.tile([P, Q], U8, name=name + "_scales", align_bytes=64)
@@ -101,16 +94,32 @@ def tile_attend_pagesaliency_kernel(tc, query, keys_words, keys_scales, gout, va
             return codes, scales
 
         def product(rows, picked, plane, h, name):
-            bank = psum.tile([P, HALF], F32, name=name)
+            bank = psum.tile([P, HALF], F32, name=name, tag=name)
             nc.tensor.matmul_mx(out=bank[:], lhsT=rows[0][:].bitcast(FP8X4), lhsT_scale=rows[1][:],
-                                rhs=picked[:].bitcast(FP4X4), rhs_scale=plane[:, h * HALF:(h + 1) * HALF],
+                                rhs=picked.bitcast(FP4X4), rhs_scale=plane[:, h * HALF:(h + 1) * HALF],
                                 start=True, stop=True)
             return bank
 
         q_mx = quantise(q_raw, "q")
-        a = [product(q_mx, gather_words(k_words, h, "k_pick%d" % h, "k_pick%d" % h), k_plane, h, "a%d" % h)
-             for h in range(2)]
         g_mx = quantise(g_raw, "g")
+        turned = [psum.tile([P, 2, P], F32, name="turned%d" % h, tag="a%d" % h) for h in range(2)]
+        faded_t = keep.tile([P, U // P, P], F32, name="faded_t")
+        faded = psum.tile([P, U], F32, name="faded")
+        for c in range(U // P):
+            nc.tensor.transpose(turned[c // 2][:, c % 2, :], old_sb[:, c * P:(c + 1) * P], ident[:])
+        for c in range(U // P):
+            nc.scalar.activation(faded_t[:, c, :], turned[c // 2][:, c % 2, :], ACT.Copy, scale=fade_col[:, c:c + 1])
+        for c in range(U // P):
+            nc.tensor.transpose(faded[:, c * P:(c + 1) * P], faded_t[:, c, :], ident[:])
+
+        k_plane = keep.tile([P, I], U8, name="k_plane", tag="q_grouped", align_bytes=64)
+        a = []
+        for h in range(2):
+            cols = slice(h * HALF, (h + 1) * HALF)
+            nc.vector.tensor_copy(k_plane[:, cols], k_bytes[:].indirect(half_list(h)))
+            a.append(product(q_mx, k_pick[:, cols], k_plane, h, "a%d" % h))
+        placed = keep.tile([P, U], F32, name="placed", tag="g_raw")
+        nc.gpsimd.memset(placed[:], 0.0)
 
         neg0 = keep.tile([P, 1], F32, name="neg0")
         neg = keep.tile([P, 1], F32, name="neg")
@@ -121,37 +130,20 @@ def tile_attend_pagesaliency_kernel(tc, query, keys_words, keys_scales, gout, va
                 nc.vector.tensor_scalar(negated[:], a[0][:], -1.0, None, ALU.mult, ALU.min, accum_out=neg0[:])
             else:
                 nc.vector.tensor_scalar(negated[:], a[1][:], -1.0, neg0[:], ALU.mult, ALU.min, accum_out=neg[:])
-            dp.append(product(g_mx, gather_words(v_words, h, "v_pick%d" % h, "turn%d" % h), v_plane, h, "dp%d" % h))
+            v_pick = keep.tile([P, HALF], U16, name="v_pick%d" % h, tag="turn%d" % h, align_bytes=64)
+            nc.vector.tensor_copy(v_pick[:], v_words[:].indirect(half_list(h)))
+            dp.append(product(g_mx, v_pick[:], v_plane, h, "dp%d" % h))
 
         p = []
         sums = []
         for h in range(2):
-            ph = keep.tile([P, HALF], F32, name="p%d" % h)
+            ph = keep.tile([P, HALF], F32, name="p%d" % h, tag="p%d" % h)
             sh = keep.tile([P, 1], F32, name="sum%d" % h)
             nc.scalar.activation(ph[:], a[h][:], ACT.Exp, bias=neg[:], accum_out=sh[:])
             p.append(ph)
             sums.append(sh)
         total = keep.tile([P, 1], F32, name="total")
         nc.scalar.activation(total[:], sums[0][:], ACT.Identity, bias=sums[1][:])
-        inv = keep.tile([P, 1], F32, name="inv")
-        nc.vector.reciprocal(inv[:], total[:])
-        factor = keep.tile([P, G], F32, name="factor")
-        nc.scalar.activation(factor[:], inv[:].to_broadcast([P, G]), ACT.Copy, scale=512.0)
-
-        old_sb = keep.tile([P, U], F32, name="old_sb", tag="v_bytes", align_bytes=64)
-        nc.sync.dma_start(old_sb[:], old)
-        fade_col = keep.tile([P, U // P], F32, name="fade_col", tag="k_bytes", align_bytes=64)
-        with nc.allow_non_contiguous_dma(reason="one fade value to a partition"):
-            nc.sync.dma_start(fade_col[:], fade.rearrange("o (c p) -> p (o c)", p=P))
-        turned = psum.tile([P, U // P, P], F32, name="turned")
-        faded_t = keep.tile([P, U // P, P], F32, name="faded_t")
-        faded = psum.tile([P, U], F32, name="faded")
-        for c in range(U // P):
-            nc.tensor.transpose(turned[:, c, :], old_sb[:, c * P:(c + 1) * P], ident[:])
-        for c in range(U // P):
-            nc.scalar.activation(faded_t[:, c, :], turned[:, c, :], ACT.Copy, scale=fade_col[:, c:c + 1])
-        for c in range(U // P):
-            nc.tensor.transpose(faded[:, c * P:(c + 1) * P], faded_t[:, c, :], ident[:])
 
         page_sum = keep.tile([P, G], F32, name="page_sum")
         w = []
@@ -159,6 +151,11 @@ def tile_attend_pagesaliency_kernel(tc, query, keys_words, keys_scales, gout, va
             wh = keep.tile([P, HALF], F32, name="w%d" % h)
             nc.vector.tensor_tensor(wh[:], dp[h][:], p[h][:], ALU.mult)
             w.append(wh)
+        inv = keep.tile([P, 1], F32, name="inv", tag="p1")
+        nc.vector.reciprocal(inv[:], total[:])
+        factor = keep.tile([P, G], F32, name="factor")
+        nc.scalar.activation(factor[:], inv[:].to_broadcast([P, G]), ACT.Copy, scale=512.0)
+
         for h in range(2):
             nc.vector.tensor_reduce(page_sum[:, h * G // 2:(h + 1) * G // 2],
                                     w[h][:].rearrange("q (g s) -> q g s", s=PAGE), AX.X, ALU.add,

@@ -19,10 +19,14 @@ ACT = mybir.ActivationFunctionType
 AX = mybir.AxisListType
 
 P = 128
+QUADRANT = 32
 PACK = 4
-HALF = 512
+BLOCKS = D // 32
+LIST_ROWS = 16
+HALF = I // 2
 PAGE = I // G
-ROWS = 16
+GAIN = 512.0
+TURNS = U // P
 
 
 def tile_attend_pagesaliency_kernel(tc, query, keys_words, keys_scales, gout, vals_words, vals_scales,
@@ -32,9 +36,11 @@ def tile_attend_pagesaliency_kernel(tc, query, keys_words, keys_scales, gout, va
         keep = ctx.enter_context(tc.tile_pool(name="keep", bufs=1))
         psum = ctx.enter_context(tc.psum_pool(name="psum", bufs=1))
 
-        slots = keep.tile([P, I // 16], U16, name="slots")
-        pages = keep.tile([P, G // 16], U16, name="pages")
-        nc.sync.dma_start(slots[:], offs)
+        def load_scales(src, name, first):
+            pool_bytes = keep.tile([P, T], U8, name=name, tag=name, align_bytes=64)
+            nc.sync.dma_start(pool_bytes[first:first + QUADRANT, :].bitcast(I32),
+                              src[0].bitcast(I32).unsqueeze(1).to_broadcast([BLOCKS, 2, T // 4]))
+            return pool_bytes
 
         def load_words(src, name, tag):
             pool_words = keep.tile([P, T], U16, name=name, tag=tag, align_bytes=64)
@@ -42,128 +48,127 @@ def tile_attend_pagesaliency_kernel(tc, query, keys_words, keys_scales, gout, va
             return pool_words
 
         def load_rows(src, name):
-            raw = keep.tile([P, PACK, Q], F32, name=name, tag=name)
-            nc.sync.dma_start(raw[:], src.rearrange("(p j) q -> p j q", j=PACK))
+            raw = keep.tile([P, PACK, Q], F32, name=name, tag=name, align_bytes=64)
+            nc.sync.dma_start(raw[:], src.rearrange("(r t) q -> r t q", t=PACK))
             return raw
 
-        v_bytes = keep.tile([P, T], U8, name="v_bytes", tag="v_bytes", align_bytes=64)
-        nc.sync.dma_start(v_bytes[0:32, :].bitcast(I32),
-                          vals_scales[0].bitcast(I32).unsqueeze(1).to_broadcast([ROWS, 2, T // 4]))
+        k_first, v_first = 0, 2 * QUADRANT
+        slots = keep.tile([P, I // LIST_ROWS], U16, name="slots")
+        pages = keep.tile([P, G // LIST_ROWS], U16, name="pages")
+        nc.sync.dma_start(slots[:], offs)
+        k_bytes = load_scales(keys_scales, "k_bytes", k_first)
+        v_bytes = load_scales(vals_scales, "v_bytes", v_first)
         nc.sync.dma_start(pages[:], offs2)
-        k_words = load_words(keys_words, "k_words", "k_words")
         q_raw = load_rows(query, "q_raw")
-        g_raw = load_rows(gout, "g_raw")
+        k_words = load_words(keys_words, "k_words", "k_words")
         old_sb = keep.tile([P, U], F32, name="old_sb")
         nc.sync.dma_start(old_sb[:], old)
+        g_raw = load_rows(gout, "g_raw")
+        fade_col = keep.tile([P, TURNS], F32, name="fade_col")
+        with nc.allow_non_contiguous_dma(reason="one value of fade to a partition and turn"):
+            nc.sync.dma_start(fade_col[:], fade.rearrange("o (c r) -> r (o c)", r=P))
 
-        warm = keep.tile([P, 1], F32, name="warm", tag="warm")
-        warm_out = keep.tile([P, 1], F32, name="warm_out", tag="warm_out")
-        nc.vector.memset(warm[:], 0.0)
+        warm = keep.tile([P, 1], F32, name="warm")
+        warm_out = keep.tile([P, 1], F32, name="warm_out")
+        nc.gpsimd.memset(warm[:], 0.0)
         nc.scalar.activation(warm_out[:], warm[:], ACT.Exp)
-        k_bytes = keep.tile([P, T], U8, name="k_bytes", tag="k_bytes", align_bytes=64)
-        nc.vector.memset(k_bytes[:].bitcast(I32), 0)
-        for j in range(4):
-            nc.scalar.dma_start(k_bytes[j:P:32, :].bitcast(I32), keys_scales[0, j:ROWS:4, :].bitcast(I32))
-        nc.vector.memset(v_bytes[32:64, :].bitcast(I32), 0)
-        nc.vector.memset(v_bytes[64:128, :].bitcast(I32), 0)
-        ident = keep.tile([P, P], F32, name="ident", tag="warm_out")
+
+        nc.vector.memset(k_bytes[QUADRANT:2 * QUADRANT, :].bitcast(I32), 0)
+        nc.gpsimd.memset(k_bytes[2 * QUADRANT:P, :].bitcast(I32), 0)
+        nc.vector.memset(v_bytes[3 * QUADRANT:P, :].bitcast(I32), 0)
+        nc.gpsimd.memset(v_bytes[0:2 * QUADRANT, :].bitcast(I32), 0)
+        ident = keep.tile([P, P], F32, name="ident")
         make_identity(nc, ident[:])
-        fade_col = keep.tile([P, U // P], F32, name="fade_col", tag="warm")
-        with nc.allow_non_contiguous_dma(reason="one fade value to a partition"):
-            nc.gpsimd.dma_start(fade_col[:], fade.rearrange("o (c p) -> p (o c)", p=P))
 
-        def half_list(h):
-            return slots[:, h * HALF // 16:(h + 1) * HALF // 16]
+        def gather_scales(pool_bytes, name, first):
+            picked = keep.tile([P, I], U8, name=name + "_picked", align_bytes=64)
+            nc.vector.tensor_copy(picked[:], pool_bytes[:].indirect(slots[:]))
+            plane = keep.tile([P, I], U8, name=name + "_plane", align_bytes=64)
+            for j in range(4):
+                nc.sync.dma_start(plane[j:P:4, :].bitcast(I32),
+                                  picked[first + 2 * j:first + 2 * j + QUADRANT, :].bitcast(I32))
+            return plane
 
-        v_picked = keep.tile([P, I], U8, name="v_picked", align_bytes=64)
-        nc.vector.tensor_copy(v_picked[:], v_bytes[:].indirect(slots[:]))
-        v_words = load_words(vals_words, "v_words", "v_bytes")
-        v_plane = keep.tile([P, I], U8, name="v_plane", align_bytes=64)
-        for j in range(4):
-            nc.sync.dma_start(v_plane[j:P:4, :].bitcast(I32), v_picked[2 * j:2 * j + 32, :].bitcast(I32))
-        k_pick = keep.tile([P, I], U16, name="k_pick", align_bytes=64)
-        nc.vector.tensor_copy(k_pick[:], k_words[:].indirect(slots[:]))
+        def gather_words(pool_words, h, name):
+            picked = keep.tile([P, HALF], U16, name=name, tag=name, align_bytes=64)
+            half_list = slots[:, h * HALF // LIST_ROWS:(h + 1) * HALF // LIST_ROWS]
+            nc.vector.tensor_copy(picked[:], pool_words[:].indirect(half_list))
+            return picked
 
         def quantise(raw, name):
-            grouped = keep.tile([P, Q, PACK], BF16, name=name + "_grouped", tag=name + "_grouped", align_bytes=64)
-            nc.scalar.copy(grouped[:], raw[:].rearrange("p j q -> p q j"))
+            grouped = keep.tile([P, Q, PACK], BF16, name=name + "_grouped", align_bytes=64)
+            nc.scalar.copy(grouped[:], raw[:].rearrange("r t q -> r q t"))
             codes = keep.tile([P, Q], U32, name=name + "_codes", align_bytes=64)
             scales = keep.tile([P, Q], U8, name=name + "_scales", align_bytes=64)
             nc.vector.quantize_mx(out=codes[:].bitcast(FP8X4), scales=scales[:],
-                                  in_=grouped[:].rearrange("p q j -> p (q j)"))
+                                  in_=grouped[:].rearrange("r q t -> r (q t)"))
             return codes, scales
 
-        def product(rows, picked, plane, h, name):
-            bank = psum.tile([P, HALF], F32, name=name, tag=name)
-            nc.tensor.matmul_mx(out=bank[:], lhsT=rows[0][:].bitcast(FP8X4), lhsT_scale=rows[1][:],
-                                rhs=picked.bitcast(FP4X4), rhs_scale=plane[:, h * HALF:(h + 1) * HALF],
-                                start=True, stop=True)
+        def product(rows_mx, words, plane, name):
+            codes, scales = rows_mx
+            bank = psum.tile([P, words.shape[1]], F32, name=name, tag=name)
+            nc.tensor.matmul_mx(out=bank[:], lhsT=codes[:].bitcast(FP8X4), lhsT_scale=scales[:],
+                                rhs=words.bitcast(FP4X4), rhs_scale=plane, start=True, stop=True)
             return bank
 
+        k_plane = gather_scales(k_bytes, "k", k_first)
+        v_words = load_words(vals_words, "v_words", "k_bytes")
+        v_plane = gather_scales(v_bytes, "v", v_first)
         q_mx = quantise(q_raw, "q")
         g_mx = quantise(g_raw, "g")
-        turned = [psum.tile([P, 2, P], F32, name="turned%d" % h, tag="a%d" % h) for h in range(2)]
-        faded_t = keep.tile([P, U // P, P], F32, name="faded_t")
+
+        turned = [psum.tile([P, TURNS // 2, P], F32, name="turned%d" % h, tag="a%d" % h) for h in range(2)]
+        faded_t = keep.tile([P, TURNS, P], F32, name="faded_t")
         faded = psum.tile([P, U], F32, name="faded")
-        for c in range(U // P):
+        for c in range(TURNS):
             nc.tensor.transpose(turned[c // 2][:, c % 2, :], old_sb[:, c * P:(c + 1) * P], ident[:])
-        for c in range(U // P):
+        for c in range(TURNS):
             nc.scalar.activation(faded_t[:, c, :], turned[c // 2][:, c % 2, :], ACT.Copy, scale=fade_col[:, c:c + 1])
-        for c in range(U // P):
+        for c in range(TURNS):
             nc.tensor.transpose(faded[:, c * P:(c + 1) * P], faded_t[:, c, :], ident[:])
 
-        k_plane = keep.tile([P, I], U8, name="k_plane", tag="q_grouped", align_bytes=64)
         a = []
         for h in range(2):
-            cols = slice(h * HALF, (h + 1) * HALF)
-            nc.vector.tensor_copy(k_plane[:, cols], k_bytes[:].indirect(half_list(h)))
-            a.append(product(q_mx, k_pick[:, cols], k_plane, h, "a%d" % h))
-        placed = keep.tile([P, U], F32, name="placed", tag="g_raw")
+            k_pick = gather_words(k_words, h, "k_pick%d" % h)
+            a.append(product(q_mx, k_pick[:], k_plane[:, h * HALF:(h + 1) * HALF], "a%d" % h))
+
+        placed = keep.tile([P, U], F32, name="placed", tag="g_raw", align_bytes=64)
         nc.gpsimd.memset(placed[:], 0.0)
 
-        neg0 = keep.tile([P, 1], F32, name="neg0")
-        neg = keep.tile([P, 1], F32, name="neg")
-        dp = []
-        for h in range(2):
-            negated = keep.tile([P, HALF], F32, name="negated%d" % h, tag="turn%d" % h, align_bytes=64)
-            if h == 0:
-                nc.vector.tensor_scalar(negated[:], a[0][:], -1.0, None, ALU.mult, ALU.min, accum_out=neg0[:])
-            else:
-                nc.vector.tensor_scalar(negated[:], a[1][:], -1.0, neg0[:], ALU.mult, ALU.min, accum_out=neg[:])
-            v_pick = keep.tile([P, HALF], U16, name="v_pick%d" % h, tag="turn%d" % h, align_bytes=64)
-            nc.vector.tensor_copy(v_pick[:], v_words[:].indirect(half_list(h)))
-            dp.append(product(g_mx, v_pick[:], v_plane, h, "dp%d" % h))
+        neg_max0 = keep.tile([P, 1], F32, name="neg_max0")
+        neg_max = keep.tile([P, 1], F32, name="neg_max")
+        negated = keep.tile([P, HALF], F32, name="negated", tag="v_pick1", align_bytes=64)
+        nc.vector.tensor_reduce(neg_max0[:], a[0][:], AX.X, ALU.max, negate=True)
+        nc.vector.tensor_scalar(negated[:], a[1][:], -1.0, neg_max0[:], ALU.mult, ALU.min, accum_out=neg_max[:])
+
+        pieces = [(0, 0, HALF), (1, 0, HALF // 2), (1, HALF // 2, HALF)]
+        v_pick = [gather_words(v_words, h, "v_pick%d" % h) for h in range(2)]
+        dp = [product(g_mx, v_pick[h][:, lo:hi], v_plane[:, h * HALF + lo:h * HALF + hi], "dp%d" % n)
+              for n, (h, lo, hi) in enumerate(pieces)]
 
         p = []
         sums = []
         for h in range(2):
-            ph = keep.tile([P, HALF], F32, name="p%d" % h, tag="p%d" % h)
-            sh = keep.tile([P, 1], F32, name="sum%d" % h)
-            nc.scalar.activation(ph[:], a[h][:], ACT.Exp, bias=neg[:], accum_out=sh[:])
-            p.append(ph)
-            sums.append(sh)
+            p.append(keep.tile([P, HALF], F32, name="p%d" % h, tag="p%d" % h))
+            sums.append(keep.tile([P, 1], F32, name="sum%d" % h))
+            nc.scalar.activation(p[h][:], a[h][:], ACT.Exp, bias=neg_max[:], accum_out=sums[h][:])
         total = keep.tile([P, 1], F32, name="total")
         nc.scalar.activation(total[:], sums[0][:], ACT.Identity, bias=sums[1][:])
 
+        w = [keep.tile([P, HALF], F32, name="w%d" % h) for h in range(2)]
+        for n, (h, lo, hi) in enumerate(pieces):
+            nc.vector.scalar_tensor_tensor(w[h][:, lo:hi], dp[n][:], GAIN, p[h][:, lo:hi], ALU.mult, ALU.mult)
+        inv_total = keep.tile([P, 1], F32, name="inv_total", tag="p0")
+        nc.vector.reciprocal(inv_total[:], total[:])
         page_sum = keep.tile([P, G], F32, name="page_sum")
-        w = []
-        for h in range(2):
-            wh = keep.tile([P, HALF], F32, name="w%d" % h)
-            nc.vector.tensor_tensor(wh[:], dp[h][:], p[h][:], ALU.mult)
-            w.append(wh)
-        inv = keep.tile([P, 1], F32, name="inv", tag="p1")
-        nc.vector.reciprocal(inv[:], total[:])
-        factor = keep.tile([P, G], F32, name="factor")
-        nc.scalar.activation(factor[:], inv[:].to_broadcast([P, G]), ACT.Copy, scale=512.0)
-
         for h in range(2):
             nc.vector.tensor_reduce(page_sum[:, h * G // 2:(h + 1) * G // 2],
                                     w[h][:].rearrange("q (g s) -> q g s", s=PAGE), AX.X, ALU.add,
                                     apply_absolute_value=True)
-        nc.vector.tensor_tensor(placed[:].indirect(pages[:]), page_sum[:], factor[:], ALU.mult)
+        nc.vector.tensor_copy(placed[:].indirect(pages[:]), page_sum[:])
 
-        for h in range(2):
+        for h, queue in enumerate((nc.sync, nc.scalar)):
             cols = slice(h * U // 2, (h + 1) * U // 2)
             res = keep.tile([P, U // 2], F32, name="res%d" % h)
-            nc.vector.tensor_tensor(res[:], faded[:, cols], placed[:, cols], ALU.add)
-            (nc.sync if h == 0 else nc.scalar).dma_start(out[:, cols], res[:])
+            nc.vector.scalar_tensor_tensor(res[:], placed[:, cols], inv_total[:], faded[:, cols], ALU.mult, ALU.add)
+            queue.dma_start(out[:, cols], res[:])

from contextlib import ExitStack

import concourse.mybir as mybir
from concourse.masks import make_identity

D, E, T, I, G, U, Q = 512, 512, 4096, 1024, 64, 512, 128
FLOPS = 2 * Q * I * (D + E)

F32 = mybir.dt.float32
BF16 = mybir.dt.bfloat16
I32 = mybir.dt.int32
U32 = mybir.dt.uint32
U16 = mybir.dt.uint16
U8 = mybir.dt.uint8
FP8X4 = mybir.dt.float8_e4m3fn_x4
FP4X4 = mybir.dt.float4_e2m1fn_x4
ALU = mybir.AluOpType
ACT = mybir.ActivationFunctionType
AX = mybir.AxisListType

P = 128
QUADRANT = 32
PACK = 4
BLOCKS = D // 32
LIST_ROWS = 16
HALF = I // 2
PAGE = I // G
GAIN = 512.0
TURNS = U // P


def tile_attend_pagesaliency_kernel(tc, query, keys_words, keys_scales, gout, vals_words, vals_scales,
                                     old, fade, offs, offs2, out):
    nc = tc.nc
    with ExitStack() as ctx:
        keep = ctx.enter_context(tc.tile_pool(name="keep", bufs=1))
        psum = ctx.enter_context(tc.psum_pool(name="psum", bufs=1))

        def load_scales(src, name, first):
            pool_bytes = keep.tile([P, T], U8, name=name, tag=name, align_bytes=64)
            nc.sync.dma_start(pool_bytes[first:first + QUADRANT, :].bitcast(I32),
                              src[0].bitcast(I32).unsqueeze(1).to_broadcast([BLOCKS, 2, T // 4]))
            return pool_bytes

        def load_words(src, name, tag):
            pool_words = keep.tile([P, T], U16, name=name, tag=tag, align_bytes=64)
            nc.sync.dma_start(pool_words[:].bitcast(I32), src[0].bitcast(I32))
            return pool_words

        def load_rows(src, name):
            raw = keep.tile([P, PACK, Q], F32, name=name, tag=name, align_bytes=64)
            nc.sync.dma_start(raw[:], src.rearrange("(r t) q -> r t q", t=PACK))
            return raw

        k_first, v_first = 0, 2 * QUADRANT
        slots = keep.tile([P, I // LIST_ROWS], U16, name="slots")
        pages = keep.tile([P, G // LIST_ROWS], U16, name="pages")
        nc.sync.dma_start(slots[:], offs)
        k_bytes = load_scales(keys_scales, "k_bytes", k_first)
        v_bytes = load_scales(vals_scales, "v_bytes", v_first)
        nc.sync.dma_start(pages[:], offs2)
        q_raw = load_rows(query, "q_raw")
        k_words = load_words(keys_words, "k_words", "k_words")
        old_sb = keep.tile([P, U], F32, name="old_sb")
        nc.sync.dma_start(old_sb[:], old)
        g_raw = load_rows(gout, "g_raw")
        fade_col = keep.tile([P, TURNS], F32, name="fade_col")
        with nc.allow_non_contiguous_dma(reason="one value of fade to a partition and turn"):
            nc.sync.dma_start(fade_col[:], fade.rearrange("o (c r) -> r (o c)", r=P))

        warm = keep.tile([P, 1], F32, name="warm")
        warm_out = keep.tile([P, 1], F32, name="warm_out")
        nc.gpsimd.memset(warm[:], 0.0)
        nc.scalar.activation(warm_out[:], warm[:], ACT.Exp)

        nc.vector.memset(k_bytes[QUADRANT:2 * QUADRANT, :].bitcast(I32), 0)
        nc.gpsimd.memset(k_bytes[2 * QUADRANT:P, :].bitcast(I32), 0)
        nc.vector.memset(v_bytes[3 * QUADRANT:P, :].bitcast(I32), 0)
        nc.gpsimd.memset(v_bytes[0:2 * QUADRANT, :].bitcast(I32), 0)
        ident = keep.tile([P, P], F32, name="ident")
        make_identity(nc, ident[:])

        def gather_scales(pool_bytes, name, first):
            picked = keep.tile([P, I], U8, name=name + "_picked", align_bytes=64)
            nc.vector.tensor_copy(picked[:], pool_bytes[:].indirect(slots[:]))
            plane = keep.tile([P, I], U8, name=name + "_plane", align_bytes=64)
            for j in range(4):
                nc.sync.dma_start(plane[j:P:4, :].bitcast(I32),
                                  picked[first + 2 * j:first + 2 * j + QUADRANT, :].bitcast(I32))
            return plane

        def gather_words(pool_words, h, name):
            picked = keep.tile([P, HALF], U16, name=name, tag=name, align_bytes=64)
            half_list = slots[:, h * HALF // LIST_ROWS:(h + 1) * HALF // LIST_ROWS]
            nc.vector.tensor_copy(picked[:], pool_words[:].indirect(half_list))
            return picked

        def quantise(raw, name):
            grouped = keep.tile([P, Q, PACK], BF16, name=name + "_grouped", align_bytes=64)
            nc.scalar.copy(grouped[:], raw[:].rearrange("r t q -> r q t"))
            codes = keep.tile([P, Q], U32, name=name + "_codes", align_bytes=64)
            scales = keep.tile([P, Q], U8, name=name + "_scales", align_bytes=64)
            nc.vector.quantize_mx(out=codes[:].bitcast(FP8X4), scales=scales[:],
                                  in_=grouped[:].rearrange("r q t -> r (q t)"))
            return codes, scales

        def product(rows_mx, words, plane, name):
            codes, scales = rows_mx
            bank = psum.tile([P, words.shape[1]], F32, name=name, tag=name)
            nc.tensor.matmul_mx(out=bank[:], lhsT=codes[:].bitcast(FP8X4), lhsT_scale=scales[:],
                                rhs=words.bitcast(FP4X4), rhs_scale=plane, start=True, stop=True)
            return bank

        k_plane = gather_scales(k_bytes, "k", k_first)
        v_words = load_words(vals_words, "v_words", "k_bytes")
        v_plane = gather_scales(v_bytes, "v", v_first)
        q_mx = quantise(q_raw, "q")
        g_mx = quantise(g_raw, "g")

        turned = [psum.tile([P, TURNS // 2, P], F32, name="turned%d" % h, tag="a%d" % h) for h in range(2)]
        faded_t = keep.tile([P, TURNS, P], F32, name="faded_t")
        faded = psum.tile([P, U], F32, name="faded")
        for c in range(TURNS):
            nc.tensor.transpose(turned[c // 2][:, c % 2, :], old_sb[:, c * P:(c + 1) * P], ident[:])
        for c in range(TURNS):
            nc.scalar.activation(faded_t[:, c, :], turned[c // 2][:, c % 2, :], ACT.Copy, scale=fade_col[:, c:c + 1])
        for c in range(TURNS):
            nc.tensor.transpose(faded[:, c * P:(c + 1) * P], faded_t[:, c, :], ident[:])

        a = []
        for h in range(2):
            k_pick = gather_words(k_words, h, "k_pick%d" % h)
            a.append(product(q_mx, k_pick[:], k_plane[:, h * HALF:(h + 1) * HALF], "a%d" % h))

        placed = keep.tile([P, U], F32, name="placed", tag="g_raw", align_bytes=64)
        nc.gpsimd.memset(placed[:], 0.0)

        neg_max0 = keep.tile([P, 1], F32, name="neg_max0")
        neg_max = keep.tile([P, 1], F32, name="neg_max")
        negated = keep.tile([P, HALF], F32, name="negated", tag="v_pick1", align_bytes=64)
        nc.vector.tensor_reduce(neg_max0[:], a[0][:], AX.X, ALU.max, negate=True)
        nc.vector.tensor_scalar(negated[:], a[1][:], -1.0, neg_max0[:], ALU.mult, ALU.min, accum_out=neg_max[:])

        pieces = [(0, 0, HALF), (1, 0, HALF // 2), (1, HALF // 2, HALF)]
        v_pick = [gather_words(v_words, h, "v_pick%d" % h) for h in range(2)]
        dp = [product(g_mx, v_pick[h][:, lo:hi], v_plane[:, h * HALF + lo:h * HALF + hi], "dp%d" % n)
              for n, (h, lo, hi) in enumerate(pieces)]

        p = []
        sums = []
        for h in range(2):
            p.append(keep.tile([P, HALF], F32, name="p%d" % h, tag="p%d" % h))
            sums.append(keep.tile([P, 1], F32, name="sum%d" % h))
            nc.scalar.activation(p[h][:], a[h][:], ACT.Exp, bias=neg_max[:], accum_out=sums[h][:])
        total = keep.tile([P, 1], F32, name="total")
        nc.scalar.activation(total[:], sums[0][:], ACT.Identity, bias=sums[1][:])

        w = [keep.tile([P, HALF], F32, name="w%d" % h) for h in range(2)]
        for n, (h, lo, hi) in enumerate(pieces):
            nc.vector.scalar_tensor_tensor(w[h][:, lo:hi], dp[n][:], GAIN, p[h][:, lo:hi], ALU.mult, ALU.mult)
        inv_total = keep.tile([P, 1], F32, name="inv_total", tag="p0")
        nc.vector.reciprocal(inv_total[:], total[:])
        page_sum = keep.tile([P, G], F32, name="page_sum")
        for h in range(2):
            nc.vector.tensor_reduce(page_sum[:, h * G // 2:(h + 1) * G // 2],
                                    w[h][:].rearrange("q (g s) -> q g s", s=PAGE), AX.X, ALU.add,
                                    apply_absolute_value=True)
        nc.vector.tensor_copy(placed[:].indirect(pages[:]), page_sum[:])

        for h, queue in enumerate((nc.sync, nc.scalar)):
            cols = slice(h * U // 2, (h + 1) * U // 2)
            res = keep.tile([P, U // 2], F32, name="res%d" % h)
            nc.vector.scalar_tensor_tensor(res[:], placed[:, cols], inv_total[:], faded[:, cols], ALU.mult, ALU.add)
            queue.dma_start(out[:, cols], res[:])
